import numpy as np, ml_dtypes
CORES = [71,199,95,223,103,231,111,239,119,247,127,255]
N = 12
QP = 128
def setup_inputs(rng):
    return {"q": rng.standard_normal((N, 128, QP), dtype=np.float32).astype(ml_dtypes.bfloat16), "k": rng.standard_normal((N, 128, 128), dtype=np.float32).astype(ml_dtypes.bfloat16), "v": rng.standard_normal((N, 128, 128), dtype=np.float32).astype(ml_dtypes.bfloat16)}
def setup_inputs_big(rng):
    d = setup_inputs(rng)
    for k in ("q", "k", "v"): d[k] = (d[k].astype(np.float32) * 1024.0).astype(d[k].dtype)
    return d
def setup_inputs_small(rng):
    d = setup_inputs(rng)
    for k in ("q", "k", "v"): d[k] = (d[k].astype(np.float32) * (1 / 1024.0)).astype(d[k].dtype)
    return d
def setup_inputs_apart(rng):
    d = setup_inputs(rng)
    f = (10.0 ** rng.permutation(np.linspace(-1.5, 1.5, N))).astype(np.float32).reshape(N, 1, 1)
    for k in ("q", "k", "v"): d[k] = (d[k].astype(np.float32) * f).astype(d[k].dtype)
    return d
def reference(q, k, v):
    Q, K, V = q.astype(np.float64), k.astype(np.float64), v.astype(np.float64)
    y = np.zeros((N, 128, QP))
    for r in range(N):
        S = [K[j].T @ Q[r] for j in range(N)]
        m = np.max([s.max(axis=0) for s in S], axis=0)
        y[r] = sum(V[j].T @ np.maximum(S[j] - 0.5 * m, 0.0) for j in range(N))
    return {"y": y.astype(ml_dtypes.bfloat16)}

@@ -1,0 +1,196 @@
+from concourse.bass import DstId, RemoteDMATransfer
+from concourse.mybir import AluOpType
+
+N = 12
+W = 128
+NHELP = 2
+
+SCRATCH = {
+    "qs":   ("sbuf", [128, W], "bfloat16"),
+    "Kall": ("sbuf", [128, N * W], "bfloat16"),
+    "Vall": ("sbuf", [128, N * W], "bfloat16"),
+    "P":    ("sbuf", [128, N * W], "bfloat16"),
+    "Z":    ("sbuf", [128, W + 1], "bfloat16"),
+    "I05":  ("sbuf", [128, W], "bfloat16"),
+    "cst":  ("sbuf", [128, 3 * W], "bfloat16"),
+    "R0":   ("sbuf", [128, W], "bfloat16"),
+    "R1":   ("sbuf", [128, W], "bfloat16"),
+    "tr":   ("sbuf", [128, W], "bfloat16"),
+    "Hs":   ("sbuf", [128, 2 * W], "bfloat16"),
+    "ysb":  ("sbuf", [128, W], "bfloat16"),
+    "dI":   ("dram", [W + 1, 128], "bfloat16"),
+    "S0":   ("psum", [128, 512], "float32"),
+    "S1":   ("psum", [128, 512], "float32"),
+    "S2":   ("psum", [128, 512], "float32"),
+    "ST0":  ("psum", [128, 512], "float32"),
+    "ST1":  ("psum", [128, 512], "float32"),
+    "ROW":  ("psum", [128, 512], "float32"),
+    "HB":   ("psum", [128, 512], "float32"),
+    "Y":    ("psum", [128, 512], "float32"),
+}
+SEMAPHORES = (["ldkv", "ldq", "ms", "id1", "id2", "hv", "snd", "st0", "st1", "dr", "ps", "srow", "shrow", "shb", "shs",
+               "py", "sy", "sto"]
+              + ["k%d" % j for j in range(N)] + ["v%d" % j for j in range(N)] + ["p%d" % j for j in range(N)])
+
+
+def _bits(m):
+    return bin(m).count("1")
+
+
+def _chip_cores(c, T, topo):
+    hosts = 1 + max(topo.host(x) for x in T.cores)
+    return [x for x in range(hosts * topo.CORES_PER_HOST)
+            if topo.host(x) == topo.host(c) and topo.chip(x) == topo.chip(c)]
+
+
+def _helpers(rc, T, topo):
+    others = [d for d in T.cores if d != rc]
+    ok = [x for x in _chip_cores(rc, T, topo)
+          if topo.die(x) != topo.die(rc) and all(topo.may_write(x, d) for d in others)]
+    return ok[-NHELP:]
+
+
+def _vplan():
+    per = [[] for _ in range(NHELP)]
+    ds = list(range(1, N))
+    base, extra = divmod(len(ds), NHELP)
+    pos = 0
+    for h in range(NHELP):
+        n = base + (1 if h < extra else 0)
+        per[h] = ds[pos:pos + n]
+        pos += n
+    return per
+
+
+def _sl(j):
+    return slice(j * W, (j + 1) * W)
+
+
+def _dst(d, core, topo):
+    rid, pid = topo.addr(d, core)
+    return DstId(rid=rid, pnc=pid)
+
+
+def _helper_program(g, core, T, topo, rc, h):
+    r = T.rank_of(rc)
+    dsts = [T.cores[(r + d) % N] for d in _vplan()[h]]
+    on_only = topo.mask(rc, core) & ~topo.mask(rc, dsts[0])
+    off = topo.mask(core, dsts[0])
+    g.wait_ge(T.sem.hv, _bits(on_only))
+    g.remote_dma_fused([RemoteDMATransfer(
+        dst_ids=[_dst(d, core, topo) for d in dsts], dma_engine_mask=off, remote_sem=T.sem["v%d" % r],
+        srcs=[T.Vall[:, _sl(r)]], dsts=[T.Vall[:, _sl(r)] for _ in dsts], alu_op=0)], local_sem=T.sem.snd)
+    g.wait_ge(T.sem.snd, _bits(off))
+
+
+def rank_program(g, core, T, topo):
+    r = T.rank_of(core)
+    if r is None:
+        for rc in T.cores:
+            if topo.host(rc) == topo.host(core) and topo.chip(rc) == topo.chip(core):
+                hs = _helpers(rc, T, topo)
+                if core in hs:
+                    _helper_program(g, core, T, topo, rc, hs.index(core))
+        return
+
+    sem = T.sem
+    pe, dve = g.tensor, g.vector
+    helpers = _helpers(core, T, topo)
+    kdst = [T.cores[(r + d) % N] for d in range(1, N)]
+    off = topo.mask(core, kdst[0])
+    on_only = topo.mask(core, helpers[0]) & ~off
+    noff = _bits(off)
+
+    g.sync.dma_start(T.Kall[:, _sl(r)], T.k[:]).then_inc(sem.ldkv, 16)
+    g.scalar.dma_start(T.Vall[:, _sl(r)], T.v[:]).then_inc(sem.ldkv, 16)
+    g.sync.dma_start(T.qs[:], T.q[:]).then_inc(sem.ldq, 16)
+    dve.memset(T.Z[:, 0:1], 0.5).then_inc(sem.ms, 1)
+    dve.memset(T.Z[:, 1:W + 1], 0.0).then_inc(sem.ms, 1)
+    dve.memset(T.cst[0:1, 0:W], 1.0).then_inc(sem.ms, 1)
+    dve.memset(T.cst[0:1, W:2 * W], -1.0).then_inc(sem.ms, 1)
+    g.scalar.wait_ge(sem.ms, 4)
+    g.scalar.dma_start(T.dI[:], T.Z[:]).then_inc(sem.id1, 16)
+    g.scalar.wait_ge(sem.id1, 16)
+    g.scalar.dma_start(T.I05[:], T.dI[0:128, :]).then_inc(sem.id2, 16)
+
+    g.wait_ge(sem.ldkv, 32)
+    g.remote_dma_fused([
+        RemoteDMATransfer(dst_ids=[_dst(d, core, topo) for d in kdst], dma_engine_mask=off, remote_sem=sem["k%d" % r],
+                          srcs=[T.Kall[:, _sl(r)]], dsts=[T.Kall[:, _sl(r)] for _ in kdst], alu_op=0),
+        RemoteDMATransfer(dst_ids=[_dst(x, core, topo) for x in helpers], dma_engine_mask=on_only, remote_sem=sem.hv,
+                          srcs=[T.Vall[:, _sl(r)]], dsts=[T.Vall[:, _sl(r)] for _ in helpers], alu_op=0),
+    ], local_sem=sem.snd)
+
+    korder = [r] + [(r - d) % N for d in range(1, N)]
+    Sb = [T.S0, T.S1, T.S2]
+    STb = [T.ST0, T.ST1]
+    Rb = [T.R0, T.R1]
+    stsem = [sem.st0, sem.st1]
+
+    def S_of(j):
+        return Sb[j // 4][:, (j % 4) * W:(j % 4 + 1) * W]
+
+    pe.wait_ge(sem.ldkv, 32)
+    pe.wait_ge(sem.ldq, 16)
+    for i, j in enumerate(korder):
+        if j != r:
+            pe.wait_ge(sem["k%d" % j], noff)
+        if i >= 2:
+            pe.wait_ge(sem.dr, i - 1)
+        pe.matmul(STb[i % 2][:, 0:W], T.qs[:], T.Kall[:, _sl(j)], True, True).then_inc(stsem[i % 2], 1)
+        pe.matmul(S_of(j), T.Kall[:, _sl(j)], T.qs[:], True, True).then_inc(sem.ps, 1)
+
+    ndr = 0
+    for i in range(N):
+        dve.wait_ge(stsem[i % 2], i // 2 + 1)
+        if i == 0:
+            dve.tensor_copy(Rb[0][:], STb[0][:, 0:W]).then_inc(sem.dr, 1)
+        else:
+            dve.wait_ge(sem.dr, ndr)
+            dve.tensor_tensor(Rb[i % 2][:], STb[i % 2][:, 0:W], Rb[(i - 1) % 2][:], AluOpType.max).then_inc(sem.dr, 1)
+        ndr += 1
+    src, lo, w = Rb[(N - 1) % 2], 0, W
+    pos = 0
+    while w > 1:
+        half = w // 2
+        dve.wait_ge(sem.dr, ndr)
+        dve.tensor_tensor(T.tr[:, pos:pos + half], src[:, lo:lo + half], src[:, lo + half:lo + w],
+                          AluOpType.max).then_inc(sem.dr, 1)
+        ndr += 1
+        src, lo, w = T.tr, pos, half
+        pos += half
+    mcol = T.tr[:, lo:lo + 1]
+
+    pe.wait_ge(sem.dr, ndr)
+    pe.wait_ge(sem.id2, 16)
+    pe.matmul(T.ROW[0:1, 0:W], mcol, T.I05[:], True, True).then_inc(sem.srow, 1)
+    dve.wait_ge(sem.srow, 1)
+    dve.tensor_copy(T.cst[0:1, 2 * W:3 * W], T.ROW[0:1, 0:W]).then_inc(sem.shrow, 1)
+    pe.wait_ge(sem.shrow, 1)
+    pe.wait_ge(sem.ms, 4)
+    pe.matmul(T.HB[:, 0:W], T.cst[0:1, 0:W], T.cst[0:1, 2 * W:3 * W], True, True).then_inc(sem.shb, 1)
+    pe.matmul(T.HB[:, W:2 * W], T.cst[0:1, W:2 * W], T.cst[0:1, 2 * W:3 * W], True, True).then_inc(sem.shb, 1)
+    dve.wait_ge(sem.shb, 2)
+    dve.tensor_copy(T.Hs[:], T.HB[:, 0:2 * W]).then_inc(sem.shs, 1)
+
+    plan = _vplan()
+    exp = sorted((p, h, d) for h in range(NHELP) for p, d in enumerate(plan[h]))
+    vorder = [r] + [(r - d) % N for _, _, d in exp]
+    dve.wait_ge(sem.shs, 1)
+    dve.wait_ge(sem.ps, N)
+    for j in vorder:
+        dve.tensor_tensor(T.P[:, _sl(j)], S_of(j), T.Hs[:, 0:W], AluOpType.max).then_inc(sem["p%d" % j], 1)
+
+    pe.wait_ge(sem.shs, 1)
+    for i, j in enumerate(vorder):
+        if j != r:
+            pe.wait_ge(sem["v%d" % j], noff)
+        pe.wait_ge(sem["p%d" % j], 1)
+        pe.matmul(T.Y[:, 0:W], T.Vall[:, _sl(j)], T.P[:, _sl(j)], i == 0, False).then_inc(sem.py, 1)
+        pe.matmul(T.Y[:, 0:W], T.Vall[:, _sl(j)], T.Hs[:, W:2 * W], False, i == N - 1).then_inc(sem.py, 1)
+    dve.wait_ge(sem.py, 2 * N)
+    dve.tensor_copy(T.ysb[:], T.Y[:, 0:W]).then_inc(sem.sy, 1)
+    g.sync.wait_ge(sem.sy, 1)
+    g.sync.dma_start(T.y[:], T.ysb[:]).then_inc(sem.sto, 16)
+    g.sync.wait_ge(sem.sto, 16)
+    g.wait_ge(sem.snd, noff + _bits(on_only))

@@ -4,6 +4,8 @@ from concourse.mybir import AluOpType
 N = 12
 W = 128
 NHELP = 2
+BANKS = [2, 3, 3, 4]
+NST = 4
 
 SCRATCH = {
     "qs":   ("sbuf", [128, W], "bfloat16"),
@@ -12,24 +14,22 @@ SCRATCH = {
     "P":    ("sbuf", [128, N * W], "bfloat16"),
     "Z":    ("sbuf", [128, W + 1], "bfloat16"),
     "I05":  ("sbuf", [128, W], "bfloat16"),
-    "cst":  ("sbuf", [128, 3 * W], "bfloat16"),
-    "R0":   ("sbuf", [128, W], "bfloat16"),
-    "R1":   ("sbuf", [128, W], "bfloat16"),
+    "cst":  ("sbuf", [128, 6 * W], "bfloat16"),
+    "RB":   ("sbuf", [128, (N + 1) * W], "bfloat16"),
     "tr":   ("sbuf", [128, W], "bfloat16"),
-    "Hs":   ("sbuf", [128, 2 * W], "bfloat16"),
     "ysb":  ("sbuf", [128, W], "bfloat16"),
     "dI":   ("dram", [W + 1, 128], "bfloat16"),
-    "S0":   ("psum", [128, 512], "float32"),
-    "S1":   ("psum", [128, 512], "float32"),
-    "S2":   ("psum", [128, 512], "float32"),
+    "SA":   ("psum", [128, 512], "float32"),
+    "SB":   ("psum", [128, 512], "float32"),
+    "SC":   ("psum", [128, 512], "float32"),
+    "SD":   ("psum", [128, 512], "float32"),
     "ST0":  ("psum", [128, 512], "float32"),
     "ST1":  ("psum", [128, 512], "float32"),
     "ROW":  ("psum", [128, 512], "float32"),
-    "HB":   ("psum", [128, 512], "float32"),
     "Y":    ("psum", [128, 512], "float32"),
 }
-SEMAPHORES = (["ldkv", "ldq", "ms", "id1", "id2", "hv", "snd", "st0", "st1", "dr", "ps", "srow", "shrow", "shb", "shs",
-               "py", "sy", "sto"]
+SEMAPHORES = (["ldkv", "ldq", "ms", "id1", "id2", "hv", "snd", "st0", "st1", "st2", "st3", "dra", "drb", "srow", "shrow",
+               "sb0", "sb1", "sb2", "sb3", "py", "sy", "sto"]
               + ["k%d" % j for j in range(N)] + ["v%d" % j for j in range(N)] + ["p%d" % j for j in range(N)])
 
 
@@ -100,14 +100,17 @@ def rank_program(g, core, T, topo):
     off = topo.mask(core, kdst[0])
     on_only = topo.mask(core, helpers[0]) & ~off
     noff = _bits(off)
+    negones = T.cst[0:1, 0:W]
+    hrow = T.cst[0:1, W:2 * W]
+    zero_tile = T.Z[:, 1:W + 1]
 
     g.sync.dma_start(T.Kall[:, _sl(r)], T.k[:]).then_inc(sem.ldkv, 16)
     g.scalar.dma_start(T.Vall[:, _sl(r)], T.v[:]).then_inc(sem.ldkv, 16)
     g.sync.dma_start(T.qs[:], T.q[:]).then_inc(sem.ldq, 16)
     dve.memset(T.Z[:, 0:1], 0.5).then_inc(sem.ms, 1)
     dve.memset(T.Z[:, 1:W + 1], 0.0).then_inc(sem.ms, 1)
-    dve.memset(T.cst[0:1, 0:W], 1.0).then_inc(sem.ms, 1)
-    dve.memset(T.cst[0:1, W:2 * W], -1.0).then_inc(sem.ms, 1)
+    dve.memset(negones, -1.0).then_inc(sem.ms, 1)
+    dve.memset(T.cst[0:1, 2 * W:6 * W], 0.0).then_inc(sem.ms, 1)
     g.scalar.wait_ge(sem.ms, 4)
     g.scalar.dma_start(T.dI[:], T.Z[:]).then_inc(sem.id1, 16)
     g.scalar.wait_ge(sem.id1, 16)
@@ -122,73 +125,98 @@ def rank_program(g, core, T, topo):
     ], local_sem=sem.snd)
 
     korder = [r] + [(r - d) % N for d in range(1, N)]
-    Sb = [T.S0, T.S1, T.S2]
-    STb = [T.ST0, T.ST1]
-    Rb = [T.R0, T.R1]
-    stsem = [sem.st0, sem.st1]
+    plan = _vplan()
+    exp = sorted((p, h, d) for h in range(NHELP) for p, d in enumerate(plan[h]))
+    vorder = [r] + [(r - d) % N for _, _, d in exp]
+    Sb = [T.SA, T.SB, T.SC, T.SD]
+    sbsem = [sem.sb0, sem.sb1, sem.sb2, sem.sb3]
+    place = {}
+    pos = 0
+    for b, n in enumerate(BANKS):
+        for c in range(n):
+            place[vorder[pos]] = (b, c)
+            pos += 1
 
     def S_of(j):
-        return Sb[j // 4][:, (j % 4) * W:(j % 4 + 1) * W]
+        b, c = place[j]
+        return Sb[b][:, c * W:(c + 1) * W]
 
+    STb = [T.ST0, T.ST1, T.ROW, T.Y]
+    stsem = [sem.st0, sem.st1, sem.st2, sem.st3]
+    chsem = [sem.dra, sem.drb]
+
+    pe.wait_ge(sem.ms, 4)
+    for b, n in enumerate(BANKS):
+        pe.matmul(Sb[b][:, 0:n * W], negones, T.cst[0:1, 2 * W:(2 + n) * W], True, False).then_inc(sbsem[b], 1)
     pe.wait_ge(sem.ldkv, 32)
     pe.wait_ge(sem.ldq, 16)
     for i, j in enumerate(korder):
         if j != r:
             pe.wait_ge(sem["k%d" % j], noff)
-        if i >= 2:
-            pe.wait_ge(sem.dr, i - 1)
-        pe.matmul(STb[i % 2][:, 0:W], T.qs[:], T.Kall[:, _sl(j)], True, True).then_inc(stsem[i % 2], 1)
-        pe.matmul(S_of(j), T.Kall[:, _sl(j)], T.qs[:], True, True).then_inc(sem.ps, 1)
+        if i >= NST:
+            pe.wait_ge(chsem[(i - NST) % 2], (i - NST) // 2 + 1)
+        pe.matmul(STb[i % NST][:, 0:W], T.qs[:], T.Kall[:, _sl(j)], True, True).then_inc(stsem[i % NST], 1)
+        pe.matmul(S_of(j), T.Kall[:, _sl(j)], T.qs[:], False, False).then_inc(sbsem[place[j][0]], 1)
 
-    ndr = 0
+    def rb(s):
+        return T.RB[:, s * W:(s + 1) * W]
+
+    cnt = [0, 0]
+    last = [None, None]
+    slot = 0
     for i in range(N):
-        dve.wait_ge(stsem[i % 2], i // 2 + 1)
-        if i == 0:
-            dve.tensor_copy(Rb[0][:], STb[0][:, 0:W]).then_inc(sem.dr, 1)
+        st = STb[i % NST][:, 0:W]
+        c = i % 2 if i < N - 1 else 0
+        dve.wait_ge(stsem[i % NST], i // NST + 1)
+        if last[c] is None:
+            dve.tensor_copy(rb(slot), st).then_inc(chsem[c], 1)
         else:
-            dve.wait_ge(sem.dr, ndr)
-            dve.tensor_tensor(Rb[i % 2][:], STb[i % 2][:, 0:W], Rb[(i - 1) % 2][:], AluOpType.max).then_inc(sem.dr, 1)
-        ndr += 1
-    src, lo, w = Rb[(N - 1) % 2], 0, W
+            dve.wait_ge(chsem[c], cnt[c])
+            dve.tensor_tensor(rb(slot), st, rb(last[c]), AluOpType.max).then_inc(chsem[c], 1)
+        cnt[c] += 1
+        last[c] = slot
+        slot += 1
+        if i == N - 2:
+            dve.wait_ge(chsem[0], cnt[0])
+            dve.wait_ge(chsem[1], cnt[1])
+            dve.tensor_tensor(rb(slot), rb(last[0]), rb(last[1]), AluOpType.max).then_inc(chsem[0], 1)
+            cnt[0] += 1
+            last[0] = slot
+            slot += 1
+    src, lo, w = T.RB, last[0] * W, W
     pos = 0
     while w > 1:
         half = w // 2
-        dve.wait_ge(sem.dr, ndr)
+        dve.wait_ge(chsem[0], cnt[0])
         dve.tensor_tensor(T.tr[:, pos:pos + half], src[:, lo:lo + half], src[:, lo + half:lo + w],
-                          AluOpType.max).then_inc(sem.dr, 1)
-        ndr += 1
+                          AluOpType.max).then_inc(chsem[0], 1)
+        cnt[0] += 1
         src, lo, w = T.tr, pos, half
         pos += half
     mcol = T.tr[:, lo:lo + 1]
 
-    pe.wait_ge(sem.dr, ndr)
+    pe.wait_ge(chsem[0], cnt[0])
     pe.wait_ge(sem.id2, 16)
     pe.matmul(T.ROW[0:1, 0:W], mcol, T.I05[:], True, True).then_inc(sem.srow, 1)
     dve.wait_ge(sem.srow, 1)
-    dve.tensor_copy(T.cst[0:1, 2 * W:3 * W], T.ROW[0:1, 0:W]).then_inc(sem.shrow, 1)
+    dve.tensor_copy(hrow, T.ROW[0:1, 0:W]).then_inc(sem.shrow, 1)
     pe.wait_ge(sem.shrow, 1)
-    pe.wait_ge(sem.ms, 4)
-    pe.matmul(T.HB[:, 0:W], T.cst[0:1, 0:W], T.cst[0:1, 2 * W:3 * W], True, True).then_inc(sem.shb, 1)
-    pe.matmul(T.HB[:, W:2 * W], T.cst[0:1, W:2 * W], T.cst[0:1, 2 * W:3 * W], True, True).then_inc(sem.shb, 1)
-    dve.wait_ge(sem.shb, 2)
-    dve.tensor_copy(T.Hs[:], T.HB[:, 0:2 * W]).then_inc(sem.shs, 1)
-
-    plan = _vplan()
-    exp = sorted((p, h, d) for h in range(NHELP) for p, d in enumerate(plan[h]))
-    vorder = [r] + [(r - d) % N for _, _, d in exp]
-    dve.wait_ge(sem.shs, 1)
-    dve.wait_ge(sem.ps, N)
     for j in vorder:
-        dve.tensor_tensor(T.P[:, _sl(j)], S_of(j), T.Hs[:, 0:W], AluOpType.max).then_inc(sem["p%d" % j], 1)
+        b, c = place[j]
+        pe.matmul(S_of(j), negones, hrow, False, c == BANKS[b] - 1).then_inc(sbsem[b], 1)
 
-    pe.wait_ge(sem.shs, 1)
+    for j in vorder:
+        b, c = place[j]
+        if c == 0:
+            dve.wait_ge(sbsem[b], 1 + 2 * BANKS[b])
+        dve.tensor_tensor(T.P[:, _sl(j)], S_of(j), zero_tile, AluOpType.max).then_inc(sem["p%d" % j], 1)
+
     for i, j in enumerate(vorder):
         if j != r:
             pe.wait_ge(sem["v%d" % j], noff)
         pe.wait_ge(sem["p%d" % j], 1)
-        pe.matmul(T.Y[:, 0:W], T.Vall[:, _sl(j)], T.P[:, _sl(j)], i == 0, False).then_inc(sem.py, 1)
-        pe.matmul(T.Y[:, 0:W], T.Vall[:, _sl(j)], T.Hs[:, W:2 * W], False, i == N - 1).then_inc(sem.py, 1)
-    dve.wait_ge(sem.py, 2 * N)
+        pe.matmul(T.Y[:, 0:W], T.Vall[:, _sl(j)], T.P[:, _sl(j)], i == 0, i == N - 1).then_inc(sem.py, 1)
+    dve.wait_ge(sem.py, N)
     dve.tensor_copy(T.ysb[:], T.Y[:, 0:W]).then_inc(sem.sy, 1)
     g.sync.wait_ge(sem.sy, 1)
     g.sync.dma_start(T.y[:], T.ysb[:]).then_inc(sem.sto, 16)

@@ -3,33 +3,34 @@ from concourse.mybir import AluOpType
 
 N = 12
 W = 128
-NHELP = 2
-BANKS = [2, 3, 3, 4]
+PW = 136
 NST = 4
+SPB = 4
 
 SCRATCH = {
     "qs":   ("sbuf", [128, W], "bfloat16"),
     "Kall": ("sbuf", [128, N * W], "bfloat16"),
     "Vall": ("sbuf", [128, N * W], "bfloat16"),
-    "P":    ("sbuf", [128, N * W], "bfloat16"),
-    "Z":    ("sbuf", [128, W + 1], "bfloat16"),
+    "P":    ("sbuf", [128, N * PW], "bfloat16"),
+    "HF":   ("sbuf", [128, W], "bfloat16"),
     "I05":  ("sbuf", [128, W], "bfloat16"),
-    "cst":  ("sbuf", [128, 6 * W], "bfloat16"),
-    "RB":   ("sbuf", [128, (N + 1) * W], "bfloat16"),
-    "tr":   ("sbuf", [128, W], "bfloat16"),
+    "RB":   ("sbuf", [128, N * W], "bfloat16"),
+    "MB":   ("sbuf", [128, 2 * W], "bfloat16"),
+    "H":    ("sbuf", [128, W], "bfloat16"),
+    "tmp":  ("sbuf", [128, W], "float32"),
     "ysb":  ("sbuf", [128, W], "bfloat16"),
-    "dI":   ("dram", [W + 1, 128], "bfloat16"),
-    "SA":   ("psum", [128, 512], "float32"),
-    "SB":   ("psum", [128, 512], "float32"),
-    "SC":   ("psum", [128, 512], "float32"),
-    "SD":   ("psum", [128, 512], "float32"),
+    "vd":   ("dram", [128, W], "bfloat16"),
+    "S0":   ("psum", [128, 512], "float32"),
+    "S1":   ("psum", [128, 512], "float32"),
+    "S2":   ("psum", [128, 512], "float32"),
     "ST0":  ("psum", [128, 512], "float32"),
     "ST1":  ("psum", [128, 512], "float32"),
-    "ROW":  ("psum", [128, 512], "float32"),
+    "ST2":  ("psum", [128, 512], "float32"),
+    "HB":   ("psum", [128, 512], "float32"),
     "Y":    ("psum", [128, 512], "float32"),
 }
-SEMAPHORES = (["ldkv", "ldq", "ms", "id1", "id2", "hv", "snd", "st0", "st1", "st2", "st3", "dra", "drb", "srow", "shrow",
-               "sb0", "sb1", "sb2", "sb3", "py", "sy", "sto"]
+SEMAPHORES = (["ldkv", "ldq", "ldv", "ms", "mp", "id2", "hv", "snd", "st0", "st1", "st2", "st3", "dra", "drb", "ss",
+               "sm", "srow", "shrow", "py", "sy", "sto"]
               + ["k%d" % j for j in range(N)] + ["v%d" % j for j in range(N)] + ["p%d" % j for j in range(N)])
 
 
@@ -43,23 +44,19 @@ def _chip_cores(c, T, topo):
             if topo.host(x) == topo.host(c) and topo.chip(x) == topo.chip(c)]
 
 
-def _helpers(rc, T, topo):
-    others = [d for d in T.cores if d != rc]
-    ok = [x for x in _chip_cores(rc, T, topo)
-          if topo.die(x) != topo.die(rc) and all(topo.may_write(x, d) for d in others)]
-    return ok[-NHELP:]
-
-
-def _vplan():
-    per = [[] for _ in range(NHELP)]
-    ds = list(range(1, N))
-    base, extra = divmod(len(ds), NHELP)
-    pos = 0
-    for h in range(NHELP):
-        n = base + (1 if h < extra else 0)
-        per[h] = ds[pos:pos + n]
-        pos += n
-    return per
+def _vplan(rc, T, topo):
+    r = T.rank_of(rc)
+    others = [T.cores[(r + d) % N] for d in range(1, N)]
+    helpers = [x for x in _chip_cores(rc, T, topo) if T.rank_of(x) is None and topo.die(x) != topo.die(rc)]
+    reach = {x: sum(1 for d in others if topo.may_write(x, d)) for x in helpers}
+    can = {d: [x for x in helpers if topo.may_write(x, d)] for d in others}
+    load = {x: [] for x in helpers}
+    for d in sorted(others, key=lambda e: len(can[e])):
+        x = min(can[d], key=lambda e: (len(load[e]), reach[e]))
+        load[x].append(d)
+    plan = [(x, load[x]) for x in helpers if load[x]]
+    plan.sort(key=lambda t: -len(t[1]))
+    return plan
 
 
 def _sl(j):
@@ -71,15 +68,14 @@ def _dst(d, core, topo):
     return DstId(rid=rid, pnc=pid)
 
 
-def _helper_program(g, core, T, topo, rc, h):
+def _helper_program(g, core, T, topo, rc, dsts):
     r = T.rank_of(rc)
-    dsts = [T.cores[(r + d) % N] for d in _vplan()[h]]
     on_only = topo.mask(rc, core) & ~topo.mask(rc, dsts[0])
     off = topo.mask(core, dsts[0])
     g.wait_ge(T.sem.hv, _bits(on_only))
     g.remote_dma_fused([RemoteDMATransfer(
         dst_ids=[_dst(d, core, topo) for d in dsts], dma_engine_mask=off, remote_sem=T.sem["v%d" % r],
-        srcs=[T.Vall[:, _sl(r)]], dsts=[T.Vall[:, _sl(r)] for _ in dsts], alu_op=0)], local_sem=T.sem.snd)
+        srcs=[T.vd[:]], dsts=[T.Vall[:, _sl(r)] for _ in dsts], alu_op=0)], local_sem=T.sem.snd)
     g.wait_ge(T.sem.snd, _bits(off))
 
 
@@ -88,66 +84,59 @@ def rank_program(g, core, T, topo):
     if r is None:
         for rc in T.cores:
             if topo.host(rc) == topo.host(core) and topo.chip(rc) == topo.chip(core):
-                hs = _helpers(rc, T, topo)
-                if core in hs:
-                    _helper_program(g, core, T, topo, rc, hs.index(core))
+                for x, dsts in _vplan(rc, T, topo):
+                    if x == core:
+                        _helper_program(g, core, T, topo, rc, dsts)
         return
 
     sem = T.sem
     pe, dve = g.tensor, g.vector
-    helpers = _helpers(core, T, topo)
+    helpers = [x for x, _ in _vplan(core, T, topo)]
     kdst = [T.cores[(r + d) % N] for d in range(1, N)]
     off = topo.mask(core, kdst[0])
     on_only = topo.mask(core, helpers[0]) & ~off
     noff = _bits(off)
-    negones = T.cst[0:1, 0:W]
-    hrow = T.cst[0:1, W:2 * W]
-    zero_tile = T.Z[:, 1:W + 1]
 
     g.sync.dma_start(T.Kall[:, _sl(r)], T.k[:]).then_inc(sem.ldkv, 16)
-    g.scalar.dma_start(T.Vall[:, _sl(r)], T.v[:]).then_inc(sem.ldkv, 16)
+    g.scalar.dma_start(T.vd[:], T.v[:]).then_inc(sem.ldkv, 16)
     g.sync.dma_start(T.qs[:], T.q[:]).then_inc(sem.ldq, 16)
-    dve.memset(T.Z[:, 0:1], 0.5).then_inc(sem.ms, 1)
-    dve.memset(T.Z[:, 1:W + 1], 0.0).then_inc(sem.ms, 1)
-    dve.memset(negones, -1.0).then_inc(sem.ms, 1)
-    dve.memset(T.cst[0:1, 2 * W:6 * W], 0.0).then_inc(sem.ms, 1)
-    g.scalar.wait_ge(sem.ms, 4)
-    g.scalar.dma_start(T.dI[:], T.Z[:]).then_inc(sem.id1, 16)
-    g.scalar.wait_ge(sem.id1, 16)
-    g.scalar.dma_start(T.I05[:], T.dI[0:128, :]).then_inc(sem.id2, 16)
+    g.scalar.dma_start(T.Vall[:, _sl(r)], T.v[:]).then_inc(sem.ldv, 16)
+    dve.memset(T.HF[:], 0.5).then_inc(sem.ms, 1)
+    dve.memset(T.P[:], 1.0).then_inc(sem.mp, 1)
 
     g.wait_ge(sem.ldkv, 32)
     g.remote_dma_fused([
         RemoteDMATransfer(dst_ids=[_dst(d, core, topo) for d in kdst], dma_engine_mask=off, remote_sem=sem["k%d" % r],
                           srcs=[T.Kall[:, _sl(r)]], dsts=[T.Kall[:, _sl(r)] for _ in kdst], alu_op=0),
         RemoteDMATransfer(dst_ids=[_dst(x, core, topo) for x in helpers], dma_engine_mask=on_only, remote_sem=sem.hv,
-                          srcs=[T.Vall[:, _sl(r)]], dsts=[T.Vall[:, _sl(r)] for _ in helpers], alu_op=0),
+                          srcs=[T.vd[:]], dsts=[T.vd[:] for _ in helpers], alu_op=0),
     ], local_sem=sem.snd)
+    g.wait_ge(sem.ms, 1)
+    g.affine_select(T.I05[:], T.HF[:], [[-1, W]], AluOpType.is_equal, 0.0, 0, 1).then_inc(sem.id2, 1)
 
     korder = [r] + [(r - d) % N for d in range(1, N)]
-    plan = _vplan()
-    exp = sorted((p, h, d) for h in range(NHELP) for p, d in enumerate(plan[h]))
-    vorder = [r] + [(r - d) % N for _, _, d in exp]
-    Sb = [T.SA, T.SB, T.SC, T.SD]
-    sbsem = [sem.sb0, sem.sb1, sem.sb2, sem.sb3]
-    place = {}
-    pos = 0
-    for b, n in enumerate(BANKS):
-        for c in range(n):
-            place[vorder[pos]] = (b, c)
-            pos += 1
+    when = {}
+    for s in range(N):
+        if s != r:
+            for idx, (_, ds) in enumerate(_vplan(T.cores[s], T, topo)):
+                if core in ds:
+                    when[s] = (ds.index(core) + idx, idx, (r - s) % N)
+    vorder = [r] + sorted(when, key=lambda s: when[s])
+    Sb = [T.S0, T.S1, T.S2]
+    place = {j: divmod(p, SPB) for p, j in enumerate(vorder)}
 
     def S_of(j):
         b, c = place[j]
         return Sb[b][:, c * W:(c + 1) * W]
 
-    STb = [T.ST0, T.ST1, T.ROW, T.Y]
+    STb = [T.ST0, T.ST1, T.ST2, T.HB]
     stsem = [sem.st0, sem.st1, sem.st2, sem.st3]
     chsem = [sem.dra, sem.drb]
 
-    pe.wait_ge(sem.ms, 4)
-    for b, n in enumerate(BANKS):
-        pe.matmul(Sb[b][:, 0:n * W], negones, T.cst[0:1, 2 * W:(2 + n) * W], True, False).then_inc(sbsem[b], 1)
+    def ST_of(i):
+        c = (i // NST) % 2
+        return STb[i % NST][:, c * W:(c + 1) * W]
+
     pe.wait_ge(sem.ldkv, 32)
     pe.wait_ge(sem.ldq, 16)
     for i, j in enumerate(korder):
@@ -155,70 +144,60 @@ def rank_program(g, core, T, topo):
             pe.wait_ge(sem["k%d" % j], noff)
         if i >= NST:
             pe.wait_ge(chsem[(i - NST) % 2], (i - NST) // 2 + 1)
-        pe.matmul(STb[i % NST][:, 0:W], T.qs[:], T.Kall[:, _sl(j)], True, True).then_inc(stsem[i % NST], 1)
-        pe.matmul(S_of(j), T.Kall[:, _sl(j)], T.qs[:], False, False).then_inc(sbsem[place[j][0]], 1)
+        pe.matmul(ST_of(i), T.qs[:], T.Kall[:, _sl(j)], True, True).then_inc(stsem[i % NST], 1)
+        pe.matmul(S_of(j), T.Kall[:, _sl(j)], T.qs[:], True, True).then_inc(sem.ss, 1)
 
     def rb(s):
         return T.RB[:, s * W:(s + 1) * W]
 
     cnt = [0, 0]
     last = [None, None]
-    slot = 0
-    for i in range(N):
-        st = STb[i % NST][:, 0:W]
-        c = i % 2 if i < N - 1 else 0
+    slot = N - 1
+    for i in range(N - 1):
+        c = i % 2
         dve.wait_ge(stsem[i % NST], i // NST + 1)
         if last[c] is None:
-            dve.tensor_copy(rb(slot), st).then_inc(chsem[c], 1)
+            dve.tensor_copy(rb(slot), ST_of(i)).then_inc(chsem[c], 1)
         else:
             dve.wait_ge(chsem[c], cnt[c])
-            dve.tensor_tensor(rb(slot), st, rb(last[c]), AluOpType.max).then_inc(chsem[c], 1)
+            dve.tensor_tensor(rb(slot), ST_of(i), rb(last[c]), AluOpType.max).then_inc(chsem[c], 1)
         cnt[c] += 1
         last[c] = slot
-        slot += 1
-        if i == N - 2:
-            dve.wait_ge(chsem[0], cnt[0])
-            dve.wait_ge(chsem[1], cnt[1])
-            dve.tensor_tensor(rb(slot), rb(last[0]), rb(last[1]), AluOpType.max).then_inc(chsem[0], 1)
-            cnt[0] += 1
-            last[0] = slot
-            slot += 1
-    src, lo, w = T.RB, last[0] * W, W
-    pos = 0
-    while w > 1:
-        half = w // 2
-        dve.wait_ge(chsem[0], cnt[0])
-        dve.tensor_tensor(T.tr[:, pos:pos + half], src[:, lo:lo + half], src[:, lo + half:lo + w],
-                          AluOpType.max).then_inc(chsem[0], 1)
-        cnt[0] += 1
-        src, lo, w = T.tr, pos, half
-        pos += half
-    mcol = T.tr[:, lo:lo + 1]
+        slot -= 1
+    dve.wait_ge(chsem[0], cnt[0])
+    dve.wait_ge(chsem[1], cnt[1])
+    dve.tensor_tensor(rb(0), rb(last[0]), rb(last[1]), AluOpType.max).then_inc(chsem[0], 1)
+    cnt[0] += 1
+    dve.wait_ge(stsem[(N - 1) % NST], (N - 1) // NST + 1)
+    dve.wait_ge(chsem[0], cnt[0])
+    dve.tensor_tensor_scan(T.MB[:], STb[(N - 1) % NST][:, 0:2 * W], T.RB[:, 0:2 * W], T.RB[:, 0:1],
+                           AluOpType.max, AluOpType.max).then_inc(sem.sm, 1)
 
-    pe.wait_ge(chsem[0], cnt[0])
-    pe.wait_ge(sem.id2, 16)
-    pe.matmul(T.ROW[0:1, 0:W], mcol, T.I05[:], True, True).then_inc(sem.srow, 1)
+    pe.wait_ge(sem.sm, 1)
+    pe.wait_ge(sem.id2, 1)
+    pe.matmul(T.HB[:, 0:W], T.MB[:, W:2 * W], T.I05[:], True, True).then_inc(sem.srow, 1)
     dve.wait_ge(sem.srow, 1)
-    dve.tensor_copy(hrow, T.ROW[0:1, 0:W]).then_inc(sem.shrow, 1)
-    pe.wait_ge(sem.shrow, 1)
-    for j in vorder:
-        b, c = place[j]
-        pe.matmul(S_of(j), negones, hrow, False, c == BANKS[b] - 1).then_inc(sbsem[b], 1)
+    dve.tensor_copy(T.H[:], T.HB[:, 0:W]).then_inc(sem.shrow, 1)
 
+    dve.wait_ge(sem.shrow, 1)
+    dve.wait_ge(sem.ss, N)
+    dve.wait_ge(sem.mp, 1)
     for j in vorder:
-        b, c = place[j]
-        if c == 0:
-            dve.wait_ge(sbsem[b], 1 + 2 * BANKS[b])
-        dve.tensor_tensor(T.P[:, _sl(j)], S_of(j), zero_tile, AluOpType.max).then_inc(sem["p%d" % j], 1)
+        dve.tensor_tensor(T.P[:, j * PW:j * PW + W], S_of(j), T.H[:], AluOpType.max).then_inc(sem["p%d" % j], 1)
 
+    pe.wait_ge(sem.mp, 1)
+    pe.wait_ge(sem.ldv, 16)
     for i, j in enumerate(vorder):
         if j != r:
             pe.wait_ge(sem["v%d" % j], noff)
         pe.wait_ge(sem["p%d" % j], 1)
-        pe.matmul(T.Y[:, 0:W], T.Vall[:, _sl(j)], T.P[:, _sl(j)], i == 0, i == N - 1).then_inc(sem.py, 1)
+        pe.matmul(T.Y[:, 0:W + 1], T.Vall[:, _sl(j)], T.P[:, j * PW:j * PW + W + 1], i == 0, i == N - 1).then_inc(sem.py, 1)
+
     dve.wait_ge(sem.py, N)
-    dve.tensor_copy(T.ysb[:], T.Y[:, 0:W]).then_inc(sem.sy, 1)
-    g.sync.wait_ge(sem.sy, 1)
+    dve.tensor_scalar(T.tmp[:], T.H[:], T.Y[:, W:W + 1], None, AluOpType.mult).then_inc(sem.sy, 1)
+    dve.wait_ge(sem.sy, 1)
+    dve.tensor_tensor(T.ysb[:], T.Y[:, 0:W], T.tmp[:], AluOpType.subtract).then_inc(sem.sy, 1)
+    g.sync.wait_ge(sem.sy, 2)
     g.sync.dma_start(T.y[:], T.ysb[:]).then_inc(sem.sto, 16)
     g.sync.wait_ge(sem.sto, 16)
     g.wait_ge(sem.snd, noff + _bits(on_only))

@@ -1,11 +1,13 @@
 from concourse.bass import DstId, RemoteDMATransfer
-from concourse.mybir import AluOpType
+from concourse.mybir import AluOpType, AxisListType, ActivationFunctionType
 
 N = 12
 W = 128
 PW = 136
 NST = 4
 SPB = 4
+NSB = 8
+ND = 3
 
 SCRATCH = {
     "qs":   ("sbuf", [128, W], "bfloat16"),
@@ -14,28 +16,35 @@ SCRATCH = {
     "P":    ("sbuf", [128, N * PW], "bfloat16"),
     "HF":   ("sbuf", [128, W], "bfloat16"),
     "I05":  ("sbuf", [128, W], "bfloat16"),
-    "RB":   ("sbuf", [128, N * W], "bfloat16"),
+    "RM":   ("sbuf", [128, 2 * W], "bfloat16"),
     "MB":   ("sbuf", [128, 2 * W], "bfloat16"),
-    "H":    ("sbuf", [128, W], "bfloat16"),
+    "Ssb":  ("sbuf", [128, NSB * W], "bfloat16"),
+    "Hs":   ("sbuf", [128, W], "bfloat16"),
     "tmp":  ("sbuf", [128, W], "float32"),
     "ysb":  ("sbuf", [128, W], "bfloat16"),
+    "kd":   ("dram", [128, W], "bfloat16"),
     "vd":   ("dram", [128, W], "bfloat16"),
     "S0":   ("psum", [128, 512], "float32"),
     "S1":   ("psum", [128, 512], "float32"),
     "S2":   ("psum", [128, 512], "float32"),
     "ST0":  ("psum", [128, 512], "float32"),
     "ST1":  ("psum", [128, 512], "float32"),
-    "ST2":  ("psum", [128, 512], "float32"),
     "HB":   ("psum", [128, 512], "float32"),
+    "H2":   ("psum", [128, 512], "float32"),
     "Y":    ("psum", [128, 512], "float32"),
 }
-SEMAPHORES = (["ldkv", "ldq", "ldv", "ms", "mp", "id2", "hv", "snd", "st0", "st1", "st2", "st3", "dra", "drb", "ss",
-               "sm", "srow", "shrow", "py", "sy", "sto"]
+SEMAPHORES = (["ldk", "ldvd", "ldq", "ldv", "ms", "mp", "id2", "hv", "snd", "st0", "st1", "st2", "st3", "fil", "dr", "ss",
+               "sc", "sm", "srow", "srow2", "shs", "py", "sy", "sto"]
               + ["k%d" % j for j in range(N)] + ["v%d" % j for j in range(N)] + ["p%d" % j for j in range(N)])
 
 
 def _bits(m):
     return bin(m).count("1")
+
+
+def _alternate(m):
+    on = [b for b in range(m.bit_length()) if (m >> b) & 1]
+    return sum(1 << b for b in on[::2])
 
 
 def _chip_cores(c, T, topo):
@@ -46,7 +55,7 @@ def _chip_cores(c, T, topo):
 
 def _vplan(rc, T, topo):
     r = T.rank_of(rc)
-    others = [T.cores[(r + d) % N] for d in range(1, N)]
+    others = [T.cores[(r + d) % N] for d in range(1, N - ND)]
     helpers = [x for x in _chip_cores(rc, T, topo) if T.rank_of(x) is None and topo.die(x) != topo.die(rc)]
     reach = {x: sum(1 for d in others if topo.may_write(x, d)) for x in helpers}
     can = {d: [x for x in helpers if topo.may_write(x, d)] for d in others}
@@ -57,6 +66,10 @@ def _vplan(rc, T, topo):
     plan = [(x, load[x]) for x in helpers if load[x]]
     plan.sort(key=lambda t: -len(t[1]))
     return plan
+
+
+def _fan_mask(rc, helper, far, topo):
+    return _alternate(topo.mask(rc, helper) & ~topo.mask(rc, far))
 
 
 def _sl(j):
@@ -70,9 +83,8 @@ def _dst(d, core, topo):
 
 def _helper_program(g, core, T, topo, rc, dsts):
     r = T.rank_of(rc)
-    on_only = topo.mask(rc, core) & ~topo.mask(rc, dsts[0])
     off = topo.mask(core, dsts[0])
-    g.wait_ge(T.sem.hv, _bits(on_only))
+    g.wait_ge(T.sem.hv, _bits(_fan_mask(rc, core, dsts[0], topo)))
     g.remote_dma_fused([RemoteDMATransfer(
         dst_ids=[_dst(d, core, topo) for d in dsts], dma_engine_mask=off, remote_sem=T.sem["v%d" % r],
         srcs=[T.vd[:]], dsts=[T.Vall[:, _sl(r)] for _ in dsts], alu_op=0)], local_sem=T.sem.snd)
@@ -90,26 +102,35 @@ def rank_program(g, core, T, topo):
         return
 
     sem = T.sem
-    pe, dve = g.tensor, g.vector
+    pe, dve, act = g.tensor, g.vector, g.scalar
     helpers = [x for x, _ in _vplan(core, T, topo)]
     kdst = [T.cores[(r + d) % N] for d in range(1, N)]
+    vdst = kdst[N - 1 - ND:]
     off = topo.mask(core, kdst[0])
-    on_only = topo.mask(core, helpers[0]) & ~off
+    fan = _fan_mask(core, helpers[0], kdst[0], topo)
     noff = _bits(off)
 
-    g.sync.dma_start(T.Kall[:, _sl(r)], T.k[:]).then_inc(sem.ldkv, 16)
-    g.scalar.dma_start(T.vd[:], T.v[:]).then_inc(sem.ldkv, 16)
+    g.sync.dma_start(T.kd[:], T.k[:]).then_inc(sem.ldk, 16)
+    g.scalar.dma_start(T.vd[:], T.v[:]).then_inc(sem.ldvd, 16)
     g.sync.dma_start(T.qs[:], T.q[:]).then_inc(sem.ldq, 16)
-    g.scalar.dma_start(T.Vall[:, _sl(r)], T.v[:]).then_inc(sem.ldv, 16)
+    g.scalar.dma_start(T.Kall[:, _sl(r)], T.k[:]).then_inc(sem.ldq, 16)
+    g.sync.dma_start(T.Vall[:, _sl(r)], T.v[:]).then_inc(sem.ldv, 16)
     dve.memset(T.HF[:], 0.5).then_inc(sem.ms, 1)
     dve.memset(T.P[:], 1.0).then_inc(sem.mp, 1)
 
-    g.wait_ge(sem.ldkv, 32)
+    g.wait_ge(sem.ldk, 16)
     g.remote_dma_fused([
         RemoteDMATransfer(dst_ids=[_dst(d, core, topo) for d in kdst], dma_engine_mask=off, remote_sem=sem["k%d" % r],
-                          srcs=[T.Kall[:, _sl(r)]], dsts=[T.Kall[:, _sl(r)] for _ in kdst], alu_op=0),
-        RemoteDMATransfer(dst_ids=[_dst(x, core, topo) for x in helpers], dma_engine_mask=on_only, remote_sem=sem.hv,
+                          srcs=[T.kd[:]], dsts=[T.Kall[:, _sl(r)] for _ in kdst], alu_op=0),
+    ], local_sem=sem.snd)
+    g.wait_ge(sem.ldvd, 16)
+    g.remote_dma_fused([
+        RemoteDMATransfer(dst_ids=[_dst(x, core, topo) for x in helpers], dma_engine_mask=fan, remote_sem=sem.hv,
                           srcs=[T.vd[:]], dsts=[T.vd[:] for _ in helpers], alu_op=0),
+    ], local_sem=sem.snd)
+    g.remote_dma_fused([
+        RemoteDMATransfer(dst_ids=[_dst(d, core, topo) for d in vdst], dma_engine_mask=off, remote_sem=sem["v%d" % r],
+                          srcs=[T.vd[:]], dsts=[T.Vall[:, _sl(r)] for _ in vdst], alu_op=0),
     ], local_sem=sem.snd)
     g.wait_ge(sem.ms, 1)
     g.affine_select(T.I05[:], T.HF[:], [[-1, W]], AluOpType.is_equal, 0.0, 0, 1).then_inc(sem.id2, 1)
@@ -120,70 +141,71 @@ def rank_program(g, core, T, topo):
         if s != r:
             for idx, (_, ds) in enumerate(_vplan(T.cores[s], T, topo)):
                 if core in ds:
-                    when[s] = (ds.index(core) + idx, idx, (r - s) % N)
-    vorder = [r] + sorted(when, key=lambda s: when[s])
+                    when[s] = (ds.index(core), idx, (r - s) % N)
+    byhelp = sorted(when, key=lambda s: when[s])
+    direct = [(r - d) % N for d in range(N - ND, N)]
+    cut = len(byhelp) - 2
+    vorder = [r] + byhelp[:cut] + direct + byhelp[cut:]
     Sb = [T.S0, T.S1, T.S2]
-    place = {j: divmod(p, SPB) for p, j in enumerate(vorder)}
+    place = {j: p for p, j in enumerate(korder)}
 
     def S_of(j):
-        b, c = place[j]
+        b, c = divmod(place[j], SPB)
         return Sb[b][:, c * W:(c + 1) * W]
 
-    STb = [T.ST0, T.ST1, T.ST2, T.HB]
+    STb = [T.ST0, T.ST1, T.HB, T.H2]
     stsem = [sem.st0, sem.st1, sem.st2, sem.st3]
-    chsem = [sem.dra, sem.drb]
 
     def ST_of(i):
         c = (i // NST) % 2
         return STb[i % NST][:, c * W:(c + 1) * W]
 
-    pe.wait_ge(sem.ldkv, 32)
-    pe.wait_ge(sem.ldq, 16)
+    pe.wait_ge(sem.ldq, 32)
     for i, j in enumerate(korder):
         if j != r:
             pe.wait_ge(sem["k%d" % j], noff)
         if i >= NST:
-            pe.wait_ge(chsem[(i - NST) % 2], (i - NST) // 2 + 1)
+            pe.wait_ge(sem.dr, i - NST + 1)
         pe.matmul(ST_of(i), T.qs[:], T.Kall[:, _sl(j)], True, True).then_inc(stsem[i % NST], 1)
         pe.matmul(S_of(j), T.Kall[:, _sl(j)], T.qs[:], True, True).then_inc(sem.ss, 1)
 
-    def rb(s):
-        return T.RB[:, s * W:(s + 1) * W]
+    for b in range(NSB // SPB):
+        act.wait_ge(sem.ss, (b + 1) * SPB)
+        act.activation(T.Ssb[:, b * SPB * W:(b + 1) * SPB * W], Sb[b][:], ActivationFunctionType.Copy).then_inc(sem.sc, 1)
 
-    cnt = [0, 0]
-    last = [None, None]
-    slot = N - 1
+    dve.wait_ge(stsem[0], 1)
+    dve.tensor_copy(T.RM[:, 0:W], ST_of(0)).then_inc(sem.fil, 1)
+    dve.tensor_copy(T.RM[:, W:2 * W], ST_of(0)).then_inc(sem.fil, 1)
+    dve.wait_ge(sem.fil, 2)
     for i in range(N - 1):
-        c = i % 2
         dve.wait_ge(stsem[i % NST], i // NST + 1)
-        if last[c] is None:
-            dve.tensor_copy(rb(slot), ST_of(i)).then_inc(chsem[c], 1)
-        else:
-            dve.wait_ge(chsem[c], cnt[c])
-            dve.tensor_tensor(rb(slot), ST_of(i), rb(last[c]), AluOpType.max).then_inc(chsem[c], 1)
-        cnt[c] += 1
-        last[c] = slot
-        slot -= 1
-    dve.wait_ge(chsem[0], cnt[0])
-    dve.wait_ge(chsem[1], cnt[1])
-    dve.tensor_tensor(rb(0), rb(last[0]), rb(last[1]), AluOpType.max).then_inc(chsem[0], 1)
-    cnt[0] += 1
+        dve.tensor_reduce(T.RM[:, i:i + 1], ST_of(i), AxisListType.X, AluOpType.max).then_inc(sem.dr, 1)
     dve.wait_ge(stsem[(N - 1) % NST], (N - 1) // NST + 1)
-    dve.wait_ge(chsem[0], cnt[0])
-    dve.tensor_tensor_scan(T.MB[:], STb[(N - 1) % NST][:, 0:2 * W], T.RB[:, 0:2 * W], T.RB[:, 0:1],
+    dve.wait_ge(sem.dr, N - 1)
+    dve.tensor_tensor_scan(T.MB[:], STb[(N - 1) % NST][:, 0:2 * W], T.RM[:], T.RM[:, 0:1],
                            AluOpType.max, AluOpType.max).then_inc(sem.sm, 1)
 
     pe.wait_ge(sem.sm, 1)
     pe.wait_ge(sem.id2, 1)
     pe.matmul(T.HB[:, 0:W], T.MB[:, W:2 * W], T.I05[:], True, True).then_inc(sem.srow, 1)
-    dve.wait_ge(sem.srow, 1)
-    dve.tensor_copy(T.H[:], T.HB[:, 0:W]).then_inc(sem.shrow, 1)
+    pe.matmul(T.H2[:, 0:W], T.MB[:, W:2 * W], T.I05[:], True, True).then_inc(sem.srow2, 1)
+    act.wait_ge(sem.srow2, 1)
+    act.activation(T.Hs[:], T.H2[:, 0:W], ActivationFunctionType.Copy).then_inc(sem.shs, 1)
 
-    dve.wait_ge(sem.shrow, 1)
-    dve.wait_ge(sem.ss, N)
+    dve.wait_ge(sem.srow, 1)
+    dve.wait_ge(sem.sc, NSB // SPB)
     dve.wait_ge(sem.mp, 1)
+    seen = [False]
     for j in vorder:
-        dve.tensor_tensor(T.P[:, j * PW:j * PW + W], S_of(j), T.H[:], AluOpType.max).then_inc(sem["p%d" % j], 1)
+        if place[j] < NSB:
+            dve.tensor_tensor(T.P[:, j * PW:j * PW + W], T.Ssb[:, _sl(place[j])], T.HB[:, 0:W],
+                              AluOpType.max).then_inc(sem["p%d" % j], 1)
+        else:
+            if not seen[0]:
+                dve.wait_ge(sem.shs, 1)
+                dve.wait_ge(sem.ss, N)
+                seen[0] = True
+            dve.tensor_tensor(T.P[:, j * PW:j * PW + W], S_of(j), T.Hs[:], AluOpType.max).then_inc(sem["p%d" % j], 1)
 
     pe.wait_ge(sem.mp, 1)
     pe.wait_ge(sem.ldv, 16)
@@ -194,10 +216,10 @@ def rank_program(g, core, T, topo):
         pe.matmul(T.Y[:, 0:W + 1], T.Vall[:, _sl(j)], T.P[:, j * PW:j * PW + W + 1], i == 0, i == N - 1).then_inc(sem.py, 1)
 
     dve.wait_ge(sem.py, N)
-    dve.tensor_scalar(T.tmp[:], T.H[:], T.Y[:, W:W + 1], None, AluOpType.mult).then_inc(sem.sy, 1)
+    dve.tensor_scalar(T.tmp[:], T.Hs[:], T.Y[:, W:W + 1], None, AluOpType.mult).then_inc(sem.sy, 1)
     dve.wait_ge(sem.sy, 1)
     dve.tensor_tensor(T.ysb[:], T.Y[:, 0:W], T.tmp[:], AluOpType.subtract).then_inc(sem.sy, 1)
     g.sync.wait_ge(sem.sy, 2)
     g.sync.dma_start(T.y[:], T.ysb[:]).then_inc(sem.sto, 16)
     g.sync.wait_ge(sem.sto, 16)
-    g.wait_ge(sem.snd, noff + _bits(on_only))
+    g.wait_ge(sem.snd, 2 * noff + _bits(fan))

from concourse.bass import DstId, RemoteDMATransfer
from concourse.mybir import AluOpType, AxisListType, ActivationFunctionType

N = 12
W = 128
PW = 136
NST = 4
SPB = 4
NSB = 8
ND = 3

SCRATCH = {
    "qs":   ("sbuf", [128, W], "bfloat16"),
    "Kall": ("sbuf", [128, N * W], "bfloat16"),
    "Vall": ("sbuf", [128, N * W], "bfloat16"),
    "P":    ("sbuf", [128, N * PW], "bfloat16"),
    "HF":   ("sbuf", [128, W], "bfloat16"),
    "I05":  ("sbuf", [128, W], "bfloat16"),
    "RM":   ("sbuf", [128, 2 * W], "bfloat16"),
    "MB":   ("sbuf", [128, 2 * W], "bfloat16"),
    "Ssb":  ("sbuf", [128, NSB * W], "bfloat16"),
    "Hs":   ("sbuf", [128, W], "bfloat16"),
    "tmp":  ("sbuf", [128, W], "float32"),
    "ysb":  ("sbuf", [128, W], "bfloat16"),
    "kd":   ("dram", [128, W], "bfloat16"),
    "vd":   ("dram", [128, W], "bfloat16"),
    "S0":   ("psum", [128, 512], "float32"),
    "S1":   ("psum", [128, 512], "float32"),
    "S2":   ("psum", [128, 512], "float32"),
    "ST0":  ("psum", [128, 512], "float32"),
    "ST1":  ("psum", [128, 512], "float32"),
    "HB":   ("psum", [128, 512], "float32"),
    "H2":   ("psum", [128, 512], "float32"),
    "Y":    ("psum", [128, 512], "float32"),
}
SEMAPHORES = (["ldk", "ldvd", "ldq", "ldv", "ms", "mp", "id2", "hv", "snd", "st0", "st1", "st2", "st3", "fil", "dr", "ss",
               "sc", "sm", "srow", "srow2", "shs", "py", "sy", "sto"]
              + ["k%d" % j for j in range(N)] + ["v%d" % j for j in range(N)] + ["p%d" % j for j in range(N)])


def _bits(m):
    return bin(m).count("1")


def _alternate(m):
    on = [b for b in range(m.bit_length()) if (m >> b) & 1]
    return sum(1 << b for b in on[::2])


def _chip_cores(c, T, topo):
    hosts = 1 + max(topo.host(x) for x in T.cores)
    return [x for x in range(hosts * topo.CORES_PER_HOST)
            if topo.host(x) == topo.host(c) and topo.chip(x) == topo.chip(c)]


def _vplan(rc, T, topo):
    r = T.rank_of(rc)
    others = [T.cores[(r + d) % N] for d in range(1, N - ND)]
    helpers = [x for x in _chip_cores(rc, T, topo) if T.rank_of(x) is None and topo.die(x) != topo.die(rc)]
    reach = {x: sum(1 for d in others if topo.may_write(x, d)) for x in helpers}
    can = {d: [x for x in helpers if topo.may_write(x, d)] for d in others}
    load = {x: [] for x in helpers}
    for d in sorted(others, key=lambda e: len(can[e])):
        x = min(can[d], key=lambda e: (len(load[e]), reach[e]))
        load[x].append(d)
    plan = [(x, load[x]) for x in helpers if load[x]]
    plan.sort(key=lambda t: -len(t[1]))
    return plan


def _fan_mask(rc, helper, far, topo):
    return _alternate(topo.mask(rc, helper) & ~topo.mask(rc, far))


def _sl(j):
    return slice(j * W, (j + 1) * W)


def _dst(d, core, topo):
    rid, pid = topo.addr(d, core)
    return DstId(rid=rid, pnc=pid)


def _helper_program(g, core, T, topo, rc, dsts):
    r = T.rank_of(rc)
    off = topo.mask(core, dsts[0])
    g.wait_ge(T.sem.hv, _bits(_fan_mask(rc, core, dsts[0], topo)))
    g.remote_dma_fused([RemoteDMATransfer(
        dst_ids=[_dst(d, core, topo) for d in dsts], dma_engine_mask=off, remote_sem=T.sem["v%d" % r],
        srcs=[T.vd[:]], dsts=[T.Vall[:, _sl(r)] for _ in dsts], alu_op=0)], local_sem=T.sem.snd)
    g.wait_ge(T.sem.snd, _bits(off))


def rank_program(g, core, T, topo):
    r = T.rank_of(core)
    if r is None:
        for rc in T.cores:
            if topo.host(rc) == topo.host(core) and topo.chip(rc) == topo.chip(core):
                for x, dsts in _vplan(rc, T, topo):
                    if x == core:
                        _helper_program(g, core, T, topo, rc, dsts)
        return

    sem = T.sem
    pe, dve, act = g.tensor, g.vector, g.scalar
    helpers = [x for x, _ in _vplan(core, T, topo)]
    kdst = [T.cores[(r + d) % N] for d in range(1, N)]
    vdst = kdst[N - 1 - ND:]
    off = topo.mask(core, kdst[0])
    fan = _fan_mask(core, helpers[0], kdst[0], topo)
    noff = _bits(off)

    g.sync.dma_start(T.kd[:], T.k[:]).then_inc(sem.ldk, 16)
    g.scalar.dma_start(T.vd[:], T.v[:]).then_inc(sem.ldvd, 16)
    g.sync.dma_start(T.qs[:], T.q[:]).then_inc(sem.ldq, 16)
    g.scalar.dma_start(T.Kall[:, _sl(r)], T.k[:]).then_inc(sem.ldq, 16)
    g.sync.dma_start(T.Vall[:, _sl(r)], T.v[:]).then_inc(sem.ldv, 16)
    dve.memset(T.HF[:], 0.5).then_inc(sem.ms, 1)
    dve.memset(T.P[:], 1.0).then_inc(sem.mp, 1)

    g.wait_ge(sem.ldk, 16)
    g.remote_dma_fused([
        RemoteDMATransfer(dst_ids=[_dst(d, core, topo) for d in kdst], dma_engine_mask=off, remote_sem=sem["k%d" % r],
                          srcs=[T.kd[:]], dsts=[T.Kall[:, _sl(r)] for _ in kdst], alu_op=0),
    ], local_sem=sem.snd)
    g.wait_ge(sem.ldvd, 16)
    g.remote_dma_fused([
        RemoteDMATransfer(dst_ids=[_dst(x, core, topo) for x in helpers], dma_engine_mask=fan, remote_sem=sem.hv,
                          srcs=[T.vd[:]], dsts=[T.vd[:] for _ in helpers], alu_op=0),
    ], local_sem=sem.snd)
    g.remote_dma_fused([
        RemoteDMATransfer(dst_ids=[_dst(d, core, topo) for d in vdst], dma_engine_mask=off, remote_sem=sem["v%d" % r],
                          srcs=[T.vd[:]], dsts=[T.Vall[:, _sl(r)] for _ in vdst], alu_op=0),
    ], local_sem=sem.snd)
    g.wait_ge(sem.ms, 1)
    g.affine_select(T.I05[:], T.HF[:], [[-1, W]], AluOpType.is_equal, 0.0, 0, 1).then_inc(sem.id2, 1)

    korder = [r] + [(r - d) % N for d in range(1, N)]
    when = {}
    for s in range(N):
        if s != r:
            for idx, (_, ds) in enumerate(_vplan(T.cores[s], T, topo)):
                if core in ds:
                    when[s] = (ds.index(core), idx, (r - s) % N)
    byhelp = sorted(when, key=lambda s: when[s])
    direct = [(r - d) % N for d in range(N - ND, N)]
    cut = len(byhelp) - 2
    vorder = [r] + byhelp[:cut] + direct + byhelp[cut:]
    Sb = [T.S0, T.S1, T.S2]
    place = {j: p for p, j in enumerate(korder)}

    def S_of(j):
        b, c = divmod(place[j], SPB)
        return Sb[b][:, c * W:(c + 1) * W]

    STb = [T.ST0, T.ST1, T.HB, T.H2]
    stsem = [sem.st0, sem.st1, sem.st2, sem.st3]

    def ST_of(i):
        c = (i // NST) % 2
        return STb[i % NST][:, c * W:(c + 1) * W]

    pe.wait_ge(sem.ldq, 32)
    for i, j in enumerate(korder):
        if j != r:
            pe.wait_ge(sem["k%d" % j], noff)
        if i >= NST:
            pe.wait_ge(sem.dr, i - NST + 1)
        pe.matmul(ST_of(i), T.qs[:], T.Kall[:, _sl(j)], True, True).then_inc(stsem[i % NST], 1)
        pe.matmul(S_of(j), T.Kall[:, _sl(j)], T.qs[:], True, True).then_inc(sem.ss, 1)

    for b in range(NSB // SPB):
        act.wait_ge(sem.ss, (b + 1) * SPB)
        act.activation(T.Ssb[:, b * SPB * W:(b + 1) * SPB * W], Sb[b][:], ActivationFunctionType.Copy).then_inc(sem.sc, 1)

    dve.wait_ge(stsem[0], 1)
    dve.tensor_copy(T.RM[:, 0:W], ST_of(0)).then_inc(sem.fil, 1)
    dve.tensor_copy(T.RM[:, W:2 * W], ST_of(0)).then_inc(sem.fil, 1)
    dve.wait_ge(sem.fil, 2)
    for i in range(N - 1):
        dve.wait_ge(stsem[i % NST], i // NST + 1)
        dve.tensor_reduce(T.RM[:, i:i + 1], ST_of(i), AxisListType.X, AluOpType.max).then_inc(sem.dr, 1)
    dve.wait_ge(stsem[(N - 1) % NST], (N - 1) // NST + 1)
    dve.wait_ge(sem.dr, N - 1)
    dve.tensor_tensor_scan(T.MB[:], STb[(N - 1) % NST][:, 0:2 * W], T.RM[:], T.RM[:, 0:1],
                           AluOpType.max, AluOpType.max).then_inc(sem.sm, 1)

    pe.wait_ge(sem.sm, 1)
    pe.wait_ge(sem.id2, 1)
    pe.matmul(T.HB[:, 0:W], T.MB[:, W:2 * W], T.I05[:], True, True).then_inc(sem.srow, 1)
    pe.matmul(T.H2[:, 0:W], T.MB[:, W:2 * W], T.I05[:], True, True).then_inc(sem.srow2, 1)
    act.wait_ge(sem.srow2, 1)
    act.activation(T.Hs[:], T.H2[:, 0:W], ActivationFunctionType.Copy).then_inc(sem.shs, 1)

    dve.wait_ge(sem.srow, 1)
    dve.wait_ge(sem.sc, NSB // SPB)
    dve.wait_ge(sem.mp, 1)
    seen = [False]
    for j in vorder:
        if place[j] < NSB:
            dve.tensor_tensor(T.P[:, j * PW:j * PW + W], T.Ssb[:, _sl(place[j])], T.HB[:, 0:W],
                              AluOpType.max).then_inc(sem["p%d" % j], 1)
        else:
            if not seen[0]:
                dve.wait_ge(sem.shs, 1)
                dve.wait_ge(sem.ss, N)
                seen[0] = True
            dve.tensor_tensor(T.P[:, j * PW:j * PW + W], S_of(j), T.Hs[:], AluOpType.max).then_inc(sem["p%d" % j], 1)

    pe.wait_ge(sem.mp, 1)
    pe.wait_ge(sem.ldv, 16)
    for i, j in enumerate(vorder):
        if j != r:
            pe.wait_ge(sem["v%d" % j], noff)
        pe.wait_ge(sem["p%d" % j], 1)
        pe.matmul(T.Y[:, 0:W + 1], T.Vall[:, _sl(j)], T.P[:, j * PW:j * PW + W + 1], i == 0, i == N - 1).then_inc(sem.py, 1)

    dve.wait_ge(sem.py, N)
    dve.tensor_scalar(T.tmp[:], T.Hs[:], T.Y[:, W:W + 1], None, AluOpType.mult).then_inc(sem.sy, 1)
    dve.wait_ge(sem.sy, 1)
    dve.tensor_tensor(T.ysb[:], T.Y[:, 0:W], T.tmp[:], AluOpType.subtract).then_inc(sem.sy, 1)
    g.sync.wait_ge(sem.sy, 2)
    g.sync.dma_start(T.y[:], T.ysb[:]).then_inc(sem.sto, 16)
    g.sync.wait_ge(sem.sto, 16)
    g.wait_ge(sem.snd, 2 * noff + _bits(fan))
